import numpy as np
import ml_dtypes


def mxq(x, axis, fmt="e4m3"):
    dtype, down = {"e4m3": (ml_dtypes.float8_e4m3fn, 7), "e5m2": (ml_dtypes.float8_e5m2, 14)}[fmt]
    v = np.moveaxis(np.asarray(x, np.float32).astype(ml_dtypes.bfloat16).astype(np.float64), axis, -1)
    blocks = v.reshape(v.shape[:-1] + (-1, 32))
    amax = np.abs(blocks).max(-1, keepdims=True)
    byte = np.maximum(np.where(amax > 0, np.frexp(amax)[1] - 1 + 127, 0) - down, 1)
    scale = np.exp2(byte - 127.0)
    codes = (blocks / scale).astype(np.float32).astype(dtype).astype(np.float64)
    return np.moveaxis((codes * scale).reshape(v.shape), -1, axis)


WIDE = False


def mx_kscale(k):
    if not WIDE:
        return np.ones(k)
    levels = np.array([10, -10, 5, -5, 0])
    if k % 512:
        return np.exp2(np.random.permutation(np.resize(levels, k // 32))).repeat(32)
    a = np.empty((k // 512, 16))
    for p in range(k // 512):
        a[p, :8] = np.random.permutation(np.resize(levels, 8))
        for g in range(8):
            far = levels[np.abs(levels - a[p, g]) >= 10]
            a[p, g + 8] = far[np.random.randint(len(far))]
    return np.exp2(a.ravel()).repeat(32)


def f64(x):
    return np.asarray(x).astype(np.float64)


def striped(idx):
    return np.tile(idx.reshape(-1, 16).T, (8, 1)).astype(np.uint16)


def unstriped(offs):
    return offs[:16].T.reshape(-1).astype(np.int64)


def striped8(idx):
    return np.concatenate([x.reshape(-1, 16).T for x in idx]).astype(np.uint16)


def runs(offs, k):
    lists = np.stack([offs[16 * r : 16 * r + 16].T.reshape(-1) for r in range(8)]).astype(np.int64)
    return lists[np.arange(k) % 512 // 64]


def pack_weight(w):
    k, n = w.shape
    w = f64(np.asarray(w, np.float32).astype(ml_dtypes.bfloat16)).reshape(k // 32, 32, n)
    amax = np.abs(w).max(1)
    byte = np.clip(np.where(amax > 0, np.frexp(amax)[1] - 1 + 127 - 7, 1), 1, 254)
    scaled = (w * np.exp2(127.0 - byte)[:, None, :]).reshape(k, n).astype(np.float32)
    words = np.ascontiguousarray(scaled.reshape(k // 512, 128, 4, n).transpose(0, 1, 3, 2)).astype(ml_dtypes.float8_e4m3fn).view(np.uint8)
    return words, np.ascontiguousarray(byte.astype(np.uint8).reshape(k // 512, 16, n))


def unpack_weight(words, scales):
    g, p, n, _ = words.shape
    vals = np.ascontiguousarray(words).view(ml_dtypes.float8_e4m3fn).astype(np.float64) * np.repeat(np.exp2(scales.astype(np.float64) - 127.0), 8, axis=1)[..., None]
    return vals.transpose(0, 1, 3, 2).reshape(g * 512, n)


def sigmoid(v):
    return 1.0 / (1.0 + np.exp(-np.maximum(v, -700.0)))


K, T, S, N, H, U = 512, 2048, 512, 512, 512, 1024


def setup_inputs():
    n = np.random.standard_normal
    s = mx_kscale(K)[:, None]
    u = mx_kscale(H)
    packed_xT = pack_weight(n((K, T)) * s)
    return {
        "x_words": packed_xT[0],
        "x_scales": packed_xT[1],
        "w1": (n((K, H)) / np.sqrt(K) / s).astype(np.float32),
        "w2": (n((K, H)) / np.sqrt(K) / s).astype(np.float32),
        "beta": np.repeat(np.random.uniform(0.5, 1.5, (8, S)), 64, axis=0).astype(np.float32),
        "gn": (np.random.uniform(0.5, 1.5, (H, 1)) * u[:, None]).astype(np.float32),
        "w3": (n((H, N)) / np.sqrt(H) / u[:, None]).astype(np.float32),
        "mem": n((N, U)).astype(np.float32),
        "offs": striped(np.random.permutation(T)[:S]),
        "two": striped(np.random.permutation(T)[:S]),
        "e1": striped8(np.stack([np.random.permutation(S) for _ in range(8)])),
        "e2": striped8(np.stack([np.random.permutation(S) for _ in range(8)])),
        "slot": striped8(np.stack([np.random.permutation(U)[:S] for _ in range(8)])),
    }


def reference(x_words, x_scales, w1, w2, beta, gn, w3, mem, offs, two, e1, e2, slot):
    xq = unpack_weight(x_words, x_scales)[:, unstriped(offs)]
    y = sigmoid(mxq(f64(w1), 0, "e4m3").T @ xq)
    x_two = unpack_weight(x_words, x_scales)[:, unstriped(two)]
    c = sigmoid(mxq(f64(w2), 0, "e4m3").T @ x_two)
    nw = (f64(beta) * y) * (c[np.arange(H)[:, None], runs(e1, H)] + c[np.arange(H)[:, None], runs(e2, H)])
    z = f64(gn) * (nw - (0.75 * c))
    h = mxq(f64(w3), 0, "e4m3").T @ mxq(z, 0, "e4m3")
    out = f64(mem).copy()
    out[np.arange(N)[:, None], runs(slot, N)] = h
    return out

@@ -1,0 +1,237 @@
+from contextlib import ExitStack
+
+import concourse.mybir as mybir
+from concourse.masks import make_identity
+
+K, T, S, N, H, U = 512, 2048, 512, 512, 512, 1024
+FLOPS = 2 * K * H * S * 2 + 2 * H * N * S
+BYTES = K * T + K * T // 32 + 4 * (2 * K * H + H * N) + 4 * 8 * S + 4 * H + 2 * 4 * N * U + 5 * 2 * 128 * S // 16
+
+F32 = mybir.dt.float32
+BF16 = mybir.dt.bfloat16
+I32 = mybir.dt.int32
+U32 = mybir.dt.uint32
+U16 = mybir.dt.uint16
+U8 = mybir.dt.uint8
+FP8X4 = mybir.dt.float8_e4m3fn_x4
+MULT = mybir.AluOpType.mult
+ADD = mybir.AluOpType.add
+SIGMOID = mybir.ActivationFunctionType.Sigmoid
+
+P = 128
+PACK = 4
+BANK = 512
+UNIT = 128
+RUNS = 8
+LOSS = 0.75
+CHUNKS = ((0,), (1,), (2, 3))
+
+
+def tile_picked_sirstep_none_p_kernel(tc, x_words, x_scales, w1, w2, beta, gn, w3, mem, offs, two, e1, e2, slot, out):
+    nc = tc.nc
+    with ExitStack() as ctx:
+        keep = ctx.enter_context(tc.tile_pool(name="keep", bufs=1))
+        ring = ctx.enter_context(tc.tile_pool(name="ring", bufs=2))
+        shared = ctx.enter_context(tc.tile_pool(name="shared", bufs=1))
+        psum = ctx.enter_context(tc.psum_pool(name="psum", bufs=1))
+
+        def bank(number, shape):
+            return psum.tile(shape, F32, name="bank%d" % number)
+
+        def load_list(dram, name):
+            tile = keep.tile([P, S // 16], U16, name=name)
+            nc.sync.dma_start(tile[:], dram)
+            return tile
+
+        def load_weight(dram, name, pieces):
+            width = dram.shape[1] // pieces
+            raws = []
+            for h in range(pieces):
+                raw = keep.tile([P, PACK, width], F32, name="%s_raw%d" % (name, h), align_bytes=64)
+                nc.sync.dma_start(raw[:], dram.rearrange("(p j) c -> p j c", j=PACK)[:, :, h * width : (h + 1) * width])
+                raws.append(raw)
+            return raws
+
+        def gpsimd_cast(out, in_):
+            for m0 in range(0, out.shape[1], 32):
+                nc.gpsimd.tensor_scalar(out[:, m0 : m0 + 32], in_[:, m0 : m0 + 32], 1.0, 0.0, MULT, ADD)
+
+        def cast_weight(copies, raws, name):
+            grouped = keep.tile([P, PACK * H], BF16, name=name + "_bf16", align_bytes=64)
+            dealt = grouped[:].rearrange("p (t m j) -> p m j t", t=PACK, j=PACK)
+            m_piece = P // len(raws)
+            for h, raw in enumerate(raws):
+                copies[h](out=dealt[:, h * m_piece : (h + 1) * m_piece], in_=raw[:].rearrange("p j (m t) -> p m j t", t=PACK))
+            return grouped
+
+        def quantize(grouped, width, name, pieces, tag=None):
+            codes = keep.tile([P, width], U32, name=name + "_codes", tag=tag or name + "_codes", align_bytes=64)
+            scales = keep.tile([P, width], U8, name=name + "_scales", align_bytes=64)
+            w = width // pieces
+            for h in range(pieces):
+                nc.vector.quantize_mx(
+                    out=codes[:, h * w : (h + 1) * w].bitcast(FP8X4),
+                    scales=scales[:, h * w : (h + 1) * w],
+                    in_=grouped[:, PACK * h * w : PACK * (h + 1) * w],
+                )
+            return codes, scales
+
+        def product(acc, still, still_cols, moving, moving_cols):
+            nc.tensor.matmul_mx(
+                out=acc,
+                lhsT=still[0][:, still_cols].bitcast(FP8X4),
+                lhsT_scale=still[1][:, still_cols],
+                rhs=moving[0][:, moving_cols].bitcast(FP8X4),
+                rhs_scale=moving[1][:, moving_cols],
+                start=True,
+                stop=True,
+            )
+
+        def turned_sum(acc, first, second):
+            nc.tensor.matmul(acc, first, ident[:], start=True, stop=False, is_transpose=True)
+            nc.tensor.matmul(acc, second, ident[:], start=False, stop=True, is_transpose=True)
+
+        x_table = keep.tile([P, T], U32, name="x_table")
+        x_bytes = keep.tile([P, T], U8, name="x_bytes")
+        nc.vector.memset(x_bytes[:].bitcast(I32), 0)
+        warm = keep.tile([P, 2], F32, name="warm")
+        nc.vector.memset(warm[:, 0:1], 0.0)
+        rate_rows = keep.tile([P, S], F32, name="rate_rows")
+        nc.gpsimd.memset(rate_rows[:], 0.0)
+        ident = keep.tile([P, P], F32, name="ident")
+        make_identity(nc, ident[:])
+
+        x_rows = keep.tile([P, T], U8, name="x_rows")
+        for q in range(4):
+            nc.sync.dma_start(x_rows[32 * q : 32 * q + 4, :].bitcast(I32), x_scales[0, 4 * q : 4 * q + 4, :].bitcast(I32))
+        nc.sync.dma_start(x_table[:].bitcast(I32), x_words[0].rearrange("p n t -> p (n t)").bitcast(I32))
+        for q in range(4):
+            nc.vector.tensor_copy(x_bytes[32 * q : 32 * q + 4, :].bitcast(I32), x_rows[32 * q : 32 * q + 4, :].bitcast(I32))
+        nc.scalar.activation(warm[:, 1:2], warm[:, 0:1], SIGMOID)
+        two_l = load_list(two, "two_l")
+        w2_raw = load_weight(w2, "w2", 2)
+        offs_l = load_list(offs, "offs_l")
+        w1_raw = load_weight(w1, "w1", 2)
+        e1_l = load_list(e1, "e1_l")
+        e2_l = load_list(e2, "e2_l")
+        gain = keep.tile([P, PACK], F32, name="gain")
+        nc.sync.dma_start(gain[:], gn.rearrange("(p t) o -> p (t o)", t=PACK))
+        nc.sync.dma_start(rate_rows[0:RUNS, :], beta.rearrange("(r x) s -> r x s", r=RUNS)[:, 0, :])
+        w3_raw = load_weight(w3, "w3", 2)
+        slot_l = load_list(slot, "slot_l")
+        pages = []
+        for t in range(PACK):
+            page = keep.tile([P, U], F32, name="page%d" % t)
+            nc.sync.dma_start(page[:], mem.rearrange("(p t) u -> p t u", t=PACK)[:, t, :])
+            pages.append(page)
+
+        def pick(offsets, j0, n, name, tags):
+            lcols = slice(j0 // 16, (j0 + n) // 16)
+            words = shared.tile([P, n], U32, name=name + "_words", offset=tags[0], align_bytes=64)
+            planes = shared.tile([P, n], U8, name=name + "_planes", offset=tags[1], align_bytes=64)
+            nc.vector.tensor_copy(words[:], x_table[:].indirect(offsets[:, lcols]))
+            nc.vector.tensor_copy(planes[:], x_bytes[:].indirect(offsets[:, lcols]))
+            return words, planes
+
+        x_two = pick(two_l, 0, S, "x_two", (4096, 6144))
+        w2_q = quantize(cast_weight((nc.scalar.copy, nc.scalar.copy), w2_raw, "w2"), H, "w2", 2)
+
+        units = S // UNIT
+        c_banks = {}
+
+        def turn_logits(u, t):
+            if t == 0:
+                c_banks[u] = bank((7, 4, 2, 7)[u], [P, PACK, P])
+            nc.tensor.transpose(c_banks[u][:, t, :], logits[t][:, u * UNIT : (u + 1) * UNIT], ident[:])
+
+        logits = []
+        for t in range(PACK):
+            acc = bank(t, [P, BANK])
+            product(acc[:], w2_q, slice(t * P, (t + 1) * P), x_two, slice(0, S))
+            logit = keep.tile([P, S], F32, name="logit%d" % t)
+            (nc.scalar.copy, nc.scalar.copy, nc.scalar.copy, nc.vector.tensor_copy)[t](out=logit[:], in_=acc[:])
+            logits.append(logit)
+            turn_logits(0, t)
+
+        x_idx = [pick(offs_l, 0, S // 2, "x_idx0", (6656, 7680))]
+        w1_q = quantize(cast_weight((nc.scalar.copy, nc.vector.tensor_copy), w1_raw, "w1"), H, "w1", 1)
+        y_banks = {}
+
+        def susceptible(u):
+            y_banks[u] = bank(5 + u % 2, [P, H])
+            product(y_banks[u][:], x_idx[u // 2], slice(u % 2 * UNIT, (u % 2 + 1) * UNIT), w1_q, slice(0, H))
+
+        susceptible(0)
+        rate_bank = bank(4, [P, units, P])
+        for u in range(units):
+            nc.tensor.transpose(rate_bank[:, u, :], rate_rows[:, u * UNIT : (u + 1) * UNIT], ident[:])
+        rate = keep.tile([P, units, RUNS], F32, name="rate")
+        nc.vector.tensor_scalar(rate[:], rate_bank[:, :, 0:RUNS], -1.0 / LOSS, None, MULT)
+        loss_gain = keep.tile([P, PACK], F32, name="loss_gain")
+        nc.vector.tensor_scalar(loss_gain[:], gain[:], -LOSS, None, MULT)
+        w3_q = quantize(cast_weight((nc.vector.tensor_copy, nc.vector.tensor_copy), w3_raw, "w3"), N, "w3", 1)
+
+        def front(u):
+            lcols = slice(u * UNIT // 16, (u + 1) * UNIT // 16)
+            g = shared.tile([P, 2, PACK, UNIT], F32, name="g%d" % u, offset=(8192, 12288, 16384, 17408)[u], align_bytes=64)
+            contacts = bank(0, [P, PACK, P])
+            for t in range(PACK):
+                nc.scalar.activation(g[:, 0, t, :], logits[t][:].indirect(e1_l[:, lcols]), SIGMOID)
+                nc.scalar.activation(g[:, 1, t, :], logits[t][:].indirect(e2_l[:, lcols]), SIGMOID)
+                turned_sum(contacts[:, t, :], g[:, 0, t, :], g[:, 1, t, :])
+            if u > 0:
+                susceptible(u)
+                for t in range(PACK):
+                    turn_logits(u, t)
+            y = shared.tile([P, PACK, P], F32, name="y%d" % u, offset=(0, 19456, 20480, 21504)[u], align_bytes=64)
+            nc.scalar.activation(y[:].rearrange("p t m -> p (t m)"), y_banks[u][:], SIGMOID)
+            c = ring.tile([P, PACK, P], F32, name="c", bufs=1)
+            nc.scalar.activation(c[:], c_banks[u][:], SIGMOID)
+            cases = ring.tile([P, PACK, P], F32, name="cases")
+            for r in range(RUNS):
+                run = slice(16 * r, 16 * r + 16)
+                nc.vector.scalar_tensor_tensor(cases[:, :, run], contacts[:, :, run], rate[:, u, r : r + 1], y[:, :, run], MULT, MULT)
+            return c, cases
+
+        def back(u, c, cases):
+            total = bank(1, [P, PACK, UNIT])
+            terms = (c, cases) if u != 1 else (cases, c)
+            for k, term in enumerate(terms):
+                for t in range(PACK):
+                    nc.tensor.matmul(
+                        total[:, t, :], term[:, t, :], ident[:], start=(k, t) == (0, 0), stop=(k, t) == (1, PACK - 1), is_transpose=True
+                    )
+            z = keep.tile([P, UNIT * PACK], BF16, name="z%d" % u, align_bytes=64)
+            nc.vector.tensor_tensor(
+                z[:].rearrange("p (j t) -> p j t", t=PACK),
+                total[:].rearrange("p t j -> p j t"),
+                loss_gain[:].unsqueeze(1).to_broadcast([P, UNIT, PACK]),
+                MULT,
+            )
+            return quantize(z, UNIT, "z%d" % u, 1)
+
+        def write(u, z_q, tiles, number):
+            lcols = slice(u * UNIT // 16, (u + 1) * UNIT // 16)
+            acc = bank(number, [P, len(tiles), UNIT])
+            for k, t in enumerate(tiles):
+                product(acc[:, k, :], w3_q, slice(t * P, (t + 1) * P), z_q, slice(0, UNIT))
+            h = keep.tile([P, len(tiles), UNIT], F32, name="h%d_%d" % (u, tiles[0]))
+            nc.scalar.copy(out=h[:], in_=acc[:])
+            for k, t in enumerate(tiles):
+                nc.vector.tensor_copy(pages[t][:].indirect(slot_l[:, lcols]), h[:, k, :])
+
+        early, late = (0, 1, 2), (3,)
+        z_q = {}
+        ahead = front(0)
+        for u in range(units):
+            z_q[u] = back(u, *ahead)
+            if u == 0:
+                x_idx.append(pick(offs_l, S // 2, S // 2, "x_idx1", (0, 1024)))
+            if u + 1 < units:
+                ahead = front(u + 1)
+            if u > 0:
+                write(u - 1, z_q[u - 1], late, 1)
+            write(u, z_q[u], early, 3)
+        write(units - 1, z_q[units - 1], late, 0)
+        for t in range(PACK):
+            nc.sync.dma_start(out.rearrange("(p t) u -> p t u", t=PACK)[:, t, :], pages[t][:])

@@ -16,6 +16,7 @@ U8 = mybir.dt.uint8
 FP8X4 = mybir.dt.float8_e4m3fn_x4
 MULT = mybir.AluOpType.mult
 ADD = mybir.AluOpType.add
+COPY = mybir.ActivationFunctionType.Copy
 SIGMOID = mybir.ActivationFunctionType.Sigmoid
 
 P = 128
@@ -43,25 +44,18 @@ def tile_picked_sirstep_none_p_kernel(tc, x_words, x_scales, w1, w2, beta, gn, w
             nc.sync.dma_start(tile[:], dram)
             return tile
 
-        def load_weight(dram, name, pieces):
-            width = dram.shape[1] // pieces
-            raws = []
-            for h in range(pieces):
-                raw = keep.tile([P, PACK, width], F32, name="%s_raw%d" % (name, h), align_bytes=64)
-                nc.sync.dma_start(raw[:], dram.rearrange("(p j) c -> p j c", j=PACK)[:, :, h * width : (h + 1) * width])
-                raws.append(raw)
-            return raws
+        def load_weight(dram, name):
+            raw = keep.tile([P, PACK, dram.shape[1]], F32, name=name + "_raw")
+            nc.sync.dma_start(raw[:], dram.rearrange("(p j) c -> p j c", j=PACK))
+            return raw
 
-        def gpsimd_cast(out, in_):
-            for m0 in range(0, out.shape[1], 32):
-                nc.gpsimd.tensor_scalar(out[:, m0 : m0 + 32], in_[:, m0 : m0 + 32], 1.0, 0.0, MULT, ADD)
-
-        def cast_weight(copies, raws, name):
-            grouped = keep.tile([P, PACK * H], BF16, name=name + "_bf16", align_bytes=64)
+        def cast_weight(scalar_share, raw, name, place):
+            grouped = shared.tile([P, PACK * H], BF16, name=name + "_bf16", offset=place, align_bytes=64)
             dealt = grouped[:].rearrange("p (t m j) -> p m j t", t=PACK, j=PACK)
-            m_piece = P // len(raws)
-            for h, raw in enumerate(raws):
-                copies[h](out=dealt[:, h * m_piece : (h + 1) * m_piece], in_=raw[:].rearrange("p j (m t) -> p m j t", t=PACK))
+            source = raw[:].rearrange("p j (m t) -> p m j t", t=PACK)
+            if scalar_share > 0:
+                nc.scalar.copy(out=dealt[:, :scalar_share], in_=source[:, :scalar_share])
+            nc.vector.tensor_copy(out=dealt[:, scalar_share:], in_=source[:, scalar_share:])
             return grouped
 
         def quantize(grouped, width, name, pieces, tag=None):
@@ -104,20 +98,20 @@ def tile_picked_sirstep_none_p_kernel(tc, x_words, x_scales, w1, w2, beta, gn, w
         x_rows = keep.tile([P, T], U8, name="x_rows")
         for q in range(4):
             nc.sync.dma_start(x_rows[32 * q : 32 * q + 4, :].bitcast(I32), x_scales[0, 4 * q : 4 * q + 4, :].bitcast(I32))
+        two_l = load_list(two, "two_l")
+        offs_l = load_list(offs, "offs_l")
         nc.sync.dma_start(x_table[:].bitcast(I32), x_words[0].rearrange("p n t -> p (n t)").bitcast(I32))
         for q in range(4):
             nc.vector.tensor_copy(x_bytes[32 * q : 32 * q + 4, :].bitcast(I32), x_rows[32 * q : 32 * q + 4, :].bitcast(I32))
         nc.scalar.activation(warm[:, 1:2], warm[:, 0:1], SIGMOID)
-        two_l = load_list(two, "two_l")
-        w2_raw = load_weight(w2, "w2", 2)
-        offs_l = load_list(offs, "offs_l")
-        w1_raw = load_weight(w1, "w1", 2)
+        w2_raw = load_weight(w2, "w2")
+        w1_raw = load_weight(w1, "w1")
         e1_l = load_list(e1, "e1_l")
         e2_l = load_list(e2, "e2_l")
         gain = keep.tile([P, PACK], F32, name="gain")
         nc.sync.dma_start(gain[:], gn.rearrange("(p t) o -> p (t o)", t=PACK))
         nc.sync.dma_start(rate_rows[0:RUNS, :], beta.rearrange("(r x) s -> r x s", r=RUNS)[:, 0, :])
-        w3_raw = load_weight(w3, "w3", 2)
+        w3_raw = load_weight(w3, "w3")
         slot_l = load_list(slot, "slot_l")
         pages = []
         for t in range(PACK):
@@ -129,12 +123,12 @@ def tile_picked_sirstep_none_p_kernel(tc, x_words, x_scales, w1, w2, beta, gn, w
             lcols = slice(j0 // 16, (j0 + n) // 16)
             words = shared.tile([P, n], U32, name=name + "_words", offset=tags[0], align_bytes=64)
             planes = shared.tile([P, n], U8, name=name + "_planes", offset=tags[1], align_bytes=64)
-            nc.vector.tensor_copy(words[:], x_table[:].indirect(offsets[:, lcols]))
             nc.vector.tensor_copy(planes[:], x_bytes[:].indirect(offsets[:, lcols]))
+            nc.vector.tensor_copy(words[:], x_table[:].indirect(offsets[:, lcols]))
             return words, planes
 
         x_two = pick(two_l, 0, S, "x_two", (4096, 6144))
-        w2_q = quantize(cast_weight((nc.scalar.copy, nc.scalar.copy), w2_raw, "w2"), H, "w2", 2)
+        w2_q = quantize(cast_weight(44, w2_raw, "w2", 24576), H, "w2", 2)
 
         units = S // UNIT
         c_banks = {}
@@ -144,17 +138,8 @@ def tile_picked_sirstep_none_p_kernel(tc, x_words, x_scales, w1, w2, beta, gn, w
                 c_banks[u] = bank((7, 4, 2, 7)[u], [P, PACK, P])
             nc.tensor.transpose(c_banks[u][:, t, :], logits[t][:, u * UNIT : (u + 1) * UNIT], ident[:])
 
-        logits = []
-        for t in range(PACK):
-            acc = bank(t, [P, BANK])
-            product(acc[:], w2_q, slice(t * P, (t + 1) * P), x_two, slice(0, S))
-            logit = keep.tile([P, S], F32, name="logit%d" % t)
-            (nc.scalar.copy, nc.scalar.copy, nc.scalar.copy, nc.vector.tensor_copy)[t](out=logit[:], in_=acc[:])
-            logits.append(logit)
-            turn_logits(0, t)
-
-        x_idx = [pick(offs_l, 0, S // 2, "x_idx0", (6656, 7680))]
-        w1_q = quantize(cast_weight((nc.scalar.copy, nc.vector.tensor_copy), w1_raw, "w1"), H, "w1", 1)
+        x_idx = [pick(offs_l, 0, S // 2, "x_idx0", (24576, 7680))]
+        w1_q = quantize(cast_weight(0, w1_raw, "w1", 28672), H, "w1", 1)
         y_banks = {}
 
         def susceptible(u):
@@ -162,6 +147,16 @@ def tile_picked_sirstep_none_p_kernel(tc, x_words, x_scales, w1, w2, beta, gn, w
             product(y_banks[u][:], x_idx[u // 2], slice(u % 2 * UNIT, (u % 2 + 1) * UNIT), w1_q, slice(0, H))
 
         susceptible(0)
+
+        logits = []
+        for t in range(PACK):
+            acc = bank(t, [P, BANK])
+            product(acc[:], w2_q, slice(t * P, (t + 1) * P), x_two, slice(0, S))
+            logit = keep.tile([P, S], F32, name="logit%d" % t)
+            (nc.scalar.copy, nc.scalar.copy, nc.vector.tensor_copy, nc.vector.tensor_copy)[t](out=logit[:], in_=acc[:])
+            logits.append(logit)
+            turn_logits(0, t)
+
         rate_bank = bank(4, [P, units, P])
         for u in range(units):
             nc.tensor.transpose(rate_bank[:, u, :], rate_rows[:, u * UNIT : (u + 1) * UNIT], ident[:])
@@ -169,11 +164,11 @@ def tile_picked_sirstep_none_p_kernel(tc, x_words, x_scales, w1, w2, beta, gn, w
         nc.vector.tensor_scalar(rate[:], rate_bank[:, :, 0:RUNS], -1.0 / LOSS, None, MULT)
         loss_gain = keep.tile([P, PACK], F32, name="loss_gain")
         nc.vector.tensor_scalar(loss_gain[:], gain[:], -LOSS, None, MULT)
-        w3_q = quantize(cast_weight((nc.vector.tensor_copy, nc.vector.tensor_copy), w3_raw, "w3"), N, "w3", 1)
+        w3_q = quantize(cast_weight(0, w3_raw, "w3", 28672), N, "w3", 1)
 
         def front(u):
             lcols = slice(u * UNIT // 16, (u + 1) * UNIT // 16)
-            g = shared.tile([P, 2, PACK, UNIT], F32, name="g%d" % u, offset=(8192, 12288, 16384, 17408)[u], align_bytes=64)
+            g = shared.tile([P, 2, PACK, UNIT], F32, name="g%d" % u, offset=(8192, 8192, 16384, 17408)[u], align_bytes=64)
             contacts = bank(0, [P, PACK, P])
             for t in range(PACK):
                 nc.scalar.activation(g[:, 0, t, :], logits[t][:].indirect(e1_l[:, lcols]), SIGMOID)
@@ -202,36 +197,56 @@ def tile_picked_sirstep_none_p_kernel(tc, x_words, x_scales, w1, w2, beta, gn, w
                         total[:, t, :], term[:, t, :], ident[:], start=(k, t) == (0, 0), stop=(k, t) == (1, PACK - 1), is_transpose=True
                     )
             z = keep.tile([P, UNIT * PACK], BF16, name="z%d" % u, align_bytes=64)
-            nc.vector.tensor_tensor(
-                z[:].rearrange("p (j t) -> p j t", t=PACK),
-                total[:].rearrange("p t j -> p j t"),
-                loss_gain[:].unsqueeze(1).to_broadcast([P, UNIT, PACK]),
-                MULT,
-            )
+            if u == 3:
+                scaled = keep.tile([P, PACK, UNIT], BF16, name="scaled%d" % u)
+                for t in range(PACK):
+                    nc.scalar.activation(scaled[:, t, :], total[:, t, :], COPY, scale=loss_gain[:, t : t + 1])
+                nc.scalar.copy(out=z[:].rearrange("p (b i t) -> p b t i", i=4, t=PACK), in_=scaled[:].rearrange("p t (b i) -> p b t i", i=4))
+            else:
+                nc.vector.tensor_tensor(
+                    z[:].rearrange("p (j t) -> p j t", t=PACK),
+                    total[:].rearrange("p t j -> p j t"),
+                    loss_gain[:].unsqueeze(1).to_broadcast([P, UNIT, PACK]),
+                    MULT,
+                )
             return quantize(z, UNIT, "z%d" % u, 1)
 
-        def write(u, z_q, tiles, number):
-            lcols = slice(u * UNIT // 16, (u + 1) * UNIT // 16)
+        def scatter(t, h, j0, n):
+            nc.vector.tensor_copy(pages[t][:].indirect(slot_l[:, j0 // 16 : (j0 + n) // 16]), h)
+
+        def write(u, z_q, groups, number, spare=None):
+            tiles = [t for group in groups for t in group]
             acc = bank(number, [P, len(tiles), UNIT])
             for k, t in enumerate(tiles):
                 product(acc[:, k, :], w3_q, slice(t * P, (t + 1) * P), z_q, slice(0, UNIT))
-            h = keep.tile([P, len(tiles), UNIT], F32, name="h%d_%d" % (u, tiles[0]))
-            nc.scalar.copy(out=h[:], in_=acc[:])
-            for k, t in enumerate(tiles):
-                nc.vector.tensor_copy(pages[t][:].indirect(slot_l[:, lcols]), h[:, k, :])
+            for group in groups:
+                k0 = tiles.index(group[0])
+                if spare is not None and group == (PACK - 1,):
+                    nc.scalar.copy(out=spare, in_=acc[:, k0, :])
+                    continue
+                h = keep.tile([P, len(group), UNIT], F32, name="h%d_%d" % (u, group[0]))
+                nc.scalar.copy(out=h[:], in_=acc[:, k0 : k0 + len(group), :])
+                for k, t in enumerate(group):
+                    scatter(t, h[:, k, :], u * UNIT, UNIT)
 
-        early, late = (0, 1, 2), (3,)
         z_q = {}
+        last = units - 1
+        both = keep.tile([P, 2 * UNIT], F32, name="both")
         ahead = front(0)
         for u in range(units):
             z_q[u] = back(u, *ahead)
             if u == 0:
                 x_idx.append(pick(offs_l, S // 2, S // 2, "x_idx1", (0, 1024)))
-            if u + 1 < units:
+            if u < last:
                 ahead = front(u + 1)
-            if u > 0:
-                write(u - 1, z_q[u - 1], late, 1)
-            write(u, z_q[u], early, 3)
-        write(units - 1, z_q[units - 1], late, 0)
+            if 0 < u < last:
+                write(u - 1, z_q[u - 1], ((3,),), 1)
+            if u < last - 1:
+                write(u, z_q[u], ((0,), (1, 2)), 3)
+            if u == last - 1:
+                write(u, z_q[u], ((0,), (1,)), 3)
+        write(last - 1, z_q[last - 1], ((2,), (3,)), 1, both[:, :UNIT])
+        write(last, z_q[last], ((0,), (1, 2), (3,)), 3, both[:, UNIT:])
+        scatter(PACK - 1, both[:], (last - 1) * UNIT, 2 * UNIT)
         for t in range(PACK):
             nc.sync.dma_start(out.rearrange("(p t) u -> p t u", t=PACK)[:, t, :], pages[t][:])

@@ -51,8 +51,8 @@ def tile_picked_sirstep_none_p_kernel(tc, x_words, x_scales, w1, w2, beta, gn, w
 
         def cast_weight(scalar_share, raw, name, place):
             grouped = shared.tile([P, PACK * H], BF16, name=name + "_bf16", offset=place, align_bytes=64)
-            dealt = grouped[:].rearrange("p (t m j) -> p m j t", t=PACK, j=PACK)
-            source = raw[:].rearrange("p j (m t) -> p m j t", t=PACK)
+            dealt = grouped[:].rearrange("p (t m j) -> p m t j", t=PACK, j=PACK)
+            source = raw[:].rearrange("p j (m t) -> p m t j", t=PACK)
             if scalar_share > 0:
                 nc.scalar.copy(out=dealt[:, :scalar_share], in_=source[:, :scalar_share])
             nc.vector.tensor_copy(out=dealt[:, scalar_share:], in_=source[:, scalar_share:])
@@ -99,8 +99,8 @@ def tile_picked_sirstep_none_p_kernel(tc, x_words, x_scales, w1, w2, beta, gn, w
         for q in range(4):
             nc.sync.dma_start(x_rows[32 * q : 32 * q + 4, :].bitcast(I32), x_scales[0, 4 * q : 4 * q + 4, :].bitcast(I32))
         two_l = load_list(two, "two_l")
-        offs_l = load_list(offs, "offs_l")
         nc.sync.dma_start(x_table[:].bitcast(I32), x_words[0].rearrange("p n t -> p (n t)").bitcast(I32))
+        offs_l = load_list(offs, "offs_l")
         for q in range(4):
             nc.vector.tensor_copy(x_bytes[32 * q : 32 * q + 4, :].bitcast(I32), x_rows[32 * q : 32 * q + 4, :].bitcast(I32))
         nc.scalar.activation(warm[:, 1:2], warm[:, 0:1], SIGMOID)

@@ -4,8 +4,9 @@ import concourse.mybir as mybir
 from concourse.masks import make_identity
 
 K, T, S, N, H, U = 512, 2048, 512, 512, 512, 1024
+RUNS = 8
 FLOPS = 2 * K * H * S * 2 + 2 * H * N * S
-BYTES = K * T + K * T // 32 + 4 * (2 * K * H + H * N) + 4 * 8 * S + 4 * H + 2 * 4 * N * U + 5 * 2 * 128 * S // 16
+BYTES = K * T + K * T // 32 + 4 * (2 * K * H + H * N) + 4 * RUNS * S + 4 * H + 2 * 4 * N * U + 5 * 2 * 128 * S // 16
 
 F32 = mybir.dt.float32
 BF16 = mybir.dt.bfloat16
@@ -15,32 +16,61 @@ U16 = mybir.dt.uint16
 U8 = mybir.dt.uint8
 FP8X4 = mybir.dt.float8_e4m3fn_x4
 MULT = mybir.AluOpType.mult
-ADD = mybir.AluOpType.add
 COPY = mybir.ActivationFunctionType.Copy
 SIGMOID = mybir.ActivationFunctionType.Sigmoid
 
 P = 128
 PACK = 4
-BANK = 512
 UNIT = 128
-RUNS = 8
+UNITS = S // UNIT
+LAST = UNITS - 1
+GROUP = 16
 LOSS = 0.75
-CHUNKS = ((0,), (1,), (2, 3))
+W2_SCALAR_SHARE = 44
+
+KB = 1024
+Y_FIRST = 0
+IDX_LATE_WORDS, IDX_LATE_BYTES = Y_FIRST, Y_FIRST + KB
+TWO_WORDS, TWO_BYTES, IDX_EARLY_BYTES = 4 * KB, 6 * KB, 7 * KB + 512
+C_FIRST = 8 * KB
+SHARES_AT = (9 * KB, 10 * KB, 16 * KB, 17 * KB)
+Y_AT = (Y_FIRST, 19 * KB, 20 * KB, 21 * KB)
+W2_AT, W1_AT = 24 * KB, 28 * KB
+IDX_EARLY_WORDS, W3_AT, CASES_FIRST = W2_AT, W1_AT, W1_AT
+GAIN_AT = 36 * KB
+HELD_AT = GAIN_AT + KB
+Z_AT = tuple(42 * KB + 4 * KB * u for u in range(UNITS))
+C_AT = (C_FIRST, Z_AT[0] + KB // 2 - 2 * KB, Z_AT[1] + KB // 2 - 2 * KB, SHARES_AT[LAST])
+CASES_AT = (CASES_FIRST, Z_AT[0] + KB // 2, Z_AT[1] + KB // 2, Z_AT[2] + KB // 2)
+
+CONTACTS_BANK = 0
+TOTAL_BANK = 1
+FIRST_BANK = 2
+MIDDLE_BANK = 3
+RATE_BANK = 4
+Y_BANK = 5
+TURNED_BANK = 6
+TURNED_FIRST_BANK = 7
 
 
 def tile_picked_sirstep_none_p_kernel(tc, x_words, x_scales, w1, w2, beta, gn, w3, mem, offs, two, e1, e2, slot, out):
     nc = tc.nc
     with ExitStack() as ctx:
         keep = ctx.enter_context(tc.tile_pool(name="keep", bufs=1))
-        ring = ctx.enter_context(tc.tile_pool(name="ring", bufs=2))
         shared = ctx.enter_context(tc.tile_pool(name="shared", bufs=1))
         psum = ctx.enter_context(tc.psum_pool(name="psum", bufs=1))
 
         def bank(number, shape):
             return psum.tile(shape, F32, name="bank%d" % number)
 
+        def placed(shape, dtype, name, place):
+            return shared.tile(shape, dtype, name=name, offset=place, align_bytes=64)
+
+        def entries(list_tile, j0, n):
+            return list_tile[:, j0 // GROUP : (j0 + n) // GROUP]
+
         def load_list(dram, name):
-            tile = keep.tile([P, S // 16], U16, name=name)
+            tile = keep.tile([P, S // GROUP], U16, name=name)
             nc.sync.dma_start(tile[:], dram)
             return tile
 
@@ -49,26 +79,27 @@ def tile_picked_sirstep_none_p_kernel(tc, x_words, x_scales, w1, w2, beta, gn, w
             nc.sync.dma_start(raw[:], dram.rearrange("(p j) c -> p j c", j=PACK))
             return raw
 
-        def cast_weight(scalar_share, raw, name, place):
-            grouped = shared.tile([P, PACK * H], BF16, name=name + "_bf16", offset=place, align_bytes=64)
+        def cast_views(raw, name, place):
+            grouped = placed([P, PACK * H], BF16, name + "_bf16", place)
             dealt = grouped[:].rearrange("p (t m j) -> p m t j", t=PACK, j=PACK)
-            source = raw[:].rearrange("p j (m t) -> p m t j", t=PACK)
-            if scalar_share > 0:
-                nc.scalar.copy(out=dealt[:, :scalar_share], in_=source[:, :scalar_share])
-            nc.vector.tensor_copy(out=dealt[:, scalar_share:], in_=source[:, scalar_share:])
-            return grouped
+            return grouped, dealt, raw[:].rearrange("p j (m t) -> p m t j", t=PACK)
 
-        def quantize(grouped, width, name, pieces, tag=None):
-            codes = keep.tile([P, width], U32, name=name + "_codes", tag=tag or name + "_codes", align_bytes=64)
+        def quantize(grouped, width, name, pieces):
+            codes = keep.tile([P, width], U32, name=name + "_codes", align_bytes=64)
             scales = keep.tile([P, width], U8, name=name + "_scales", align_bytes=64)
-            w = width // pieces
-            for h in range(pieces):
+            piece = width // pieces
+            for c0 in range(0, width, piece):
                 nc.vector.quantize_mx(
-                    out=codes[:, h * w : (h + 1) * w].bitcast(FP8X4),
-                    scales=scales[:, h * w : (h + 1) * w],
-                    in_=grouped[:, PACK * h * w : PACK * (h + 1) * w],
+                    out=codes[:, c0 : c0 + piece].bitcast(FP8X4),
+                    scales=scales[:, c0 : c0 + piece],
+                    in_=grouped[:, PACK * c0 : PACK * (c0 + piece)],
                 )
             return codes, scales
+
+        def quantize_on_vector(raw, name, place):
+            grouped, dealt, source = cast_views(raw, name, place)
+            nc.vector.tensor_copy(out=dealt, in_=source)
+            return quantize(grouped, H, name, 1)
 
         def product(acc, still, still_cols, moving, moving_cols):
             nc.tensor.matmul_mx(
@@ -81,9 +112,11 @@ def tile_picked_sirstep_none_p_kernel(tc, x_words, x_scales, w1, w2, beta, gn, w
                 stop=True,
             )
 
-        def turned_sum(acc, first, second):
-            nc.tensor.matmul(acc, first, ident[:], start=True, stop=False, is_transpose=True)
-            nc.tensor.matmul(acc, second, ident[:], start=False, stop=True, is_transpose=True)
+        def turn(acc, block, start, stop):
+            nc.tensor.matmul(acc, block, ident[:], start=start, stop=stop, is_transpose=True)
+
+        def quarter(t):
+            return slice(t * P, (t + 1) * P)
 
         x_table = keep.tile([P, T], U32, name="x_table")
         x_bytes = keep.tile([P, T], U8, name="x_bytes")
@@ -105,12 +138,12 @@ def tile_picked_sirstep_none_p_kernel(tc, x_words, x_scales, w1, w2, beta, gn, w
             nc.vector.tensor_copy(x_bytes[32 * q : 32 * q + 4, :].bitcast(I32), x_rows[32 * q : 32 * q + 4, :].bitcast(I32))
         nc.scalar.activation(warm[:, 1:2], warm[:, 0:1], SIGMOID)
         w2_raw = load_weight(w2, "w2")
-        w1_raw = load_weight(w1, "w1")
-        e1_l = load_list(e1, "e1_l")
-        e2_l = load_list(e2, "e2_l")
         gain = keep.tile([P, PACK], F32, name="gain")
         nc.sync.dma_start(gain[:], gn.rearrange("(p t) o -> p (t o)", t=PACK))
         nc.sync.dma_start(rate_rows[0:RUNS, :], beta.rearrange("(r x) s -> r x s", r=RUNS)[:, 0, :])
+        w1_raw = load_weight(w1, "w1")
+        e1_l = load_list(e1, "e1_l")
+        e2_l = load_list(e2, "e2_l")
         w3_raw = load_weight(w3, "w3")
         slot_l = load_list(slot, "slot_l")
         pages = []
@@ -119,134 +152,134 @@ def tile_picked_sirstep_none_p_kernel(tc, x_words, x_scales, w1, w2, beta, gn, w
             nc.sync.dma_start(page[:], mem.rearrange("(p t) u -> p t u", t=PACK)[:, t, :])
             pages.append(page)
 
-        def pick(offsets, j0, n, name, tags):
-            lcols = slice(j0 // 16, (j0 + n) // 16)
-            words = shared.tile([P, n], U32, name=name + "_words", offset=tags[0], align_bytes=64)
-            planes = shared.tile([P, n], U8, name=name + "_planes", offset=tags[1], align_bytes=64)
-            nc.vector.tensor_copy(planes[:], x_bytes[:].indirect(offsets[:, lcols]))
-            nc.vector.tensor_copy(words[:], x_table[:].indirect(offsets[:, lcols]))
-            return words, planes
+        def pick(list_tile, j0, n, name, words_at, bytes_at):
+            words = placed([P, n], U32, name + "_words", words_at)
+            scale_bytes = placed([P, n], U8, name + "_bytes", bytes_at)
+            nc.vector.tensor_copy(scale_bytes[:], x_bytes[:].indirect(entries(list_tile, j0, n)))
+            nc.vector.tensor_copy(words[:], x_table[:].indirect(entries(list_tile, j0, n)))
+            return words, scale_bytes
 
-        x_two = pick(two_l, 0, S, "x_two", (4096, 6144))
-        w2_q = quantize(cast_weight(44, w2_raw, "w2", 24576), H, "w2", 2)
+        x_two = pick(two_l, 0, S, "x_two", TWO_WORDS, TWO_BYTES)
+        grouped, dealt, source = cast_views(w2_raw, "w2", W2_AT)
+        nc.scalar.copy(out=dealt[:, :W2_SCALAR_SHARE], in_=source[:, :W2_SCALAR_SHARE])
+        nc.vector.tensor_copy(out=dealt[:, W2_SCALAR_SHARE:], in_=source[:, W2_SCALAR_SHARE:])
+        w2_q = quantize(grouped, H, "w2", 2)
 
-        units = S // UNIT
+        x_idx = [pick(offs_l, 0, S // 2, "x_idx0", IDX_EARLY_WORDS, IDX_EARLY_BYTES)]
+        w1_q = quantize_on_vector(w1_raw, "w1", W1_AT)
+
+        y_banks = {}
         c_banks = {}
+        logits = []
+
+        def y_logits(u):
+            y_banks[u] = bank(Y_BANK if u < 2 else FIRST_BANK, [P, H])
+            product(y_banks[u][:], x_idx[u // 2], slice(u % 2 * UNIT, (u % 2 + 1) * UNIT), w1_q, slice(0, H))
 
         def turn_logits(u, t):
             if t == 0:
-                c_banks[u] = bank((7, 4, 2, 7)[u], [P, PACK, P])
+                c_banks[u] = bank(TURNED_BANK if u > 0 else TURNED_FIRST_BANK, [P, PACK, P])
             nc.tensor.transpose(c_banks[u][:, t, :], logits[t][:, u * UNIT : (u + 1) * UNIT], ident[:])
 
-        x_idx = [pick(offs_l, 0, S // 2, "x_idx0", (24576, 7680))]
-        w1_q = quantize(cast_weight(0, w1_raw, "w1", 28672), H, "w1", 1)
-        y_banks = {}
-
-        def susceptible(u):
-            y_banks[u] = bank(5 + u % 2, [P, H])
-            product(y_banks[u][:], x_idx[u // 2], slice(u % 2 * UNIT, (u % 2 + 1) * UNIT), w1_q, slice(0, H))
-
-        susceptible(0)
-
-        logits = []
+        y_logits(0)
         for t in range(PACK):
-            acc = bank(t, [P, BANK])
-            product(acc[:], w2_q, slice(t * P, (t + 1) * P), x_two, slice(0, S))
+            acc = bank(t, [P, S])
+            product(acc[:], w2_q, quarter(t), x_two, slice(0, S))
             logit = keep.tile([P, S], F32, name="logit%d" % t)
-            (nc.scalar.copy, nc.scalar.copy, nc.vector.tensor_copy, nc.vector.tensor_copy)[t](out=logit[:], in_=acc[:])
+            (nc.scalar.copy if t < 2 else nc.vector.tensor_copy)(out=logit[:], in_=acc[:])
             logits.append(logit)
             turn_logits(0, t)
+            turn_logits(1, t)
 
-        rate_bank = bank(4, [P, units, P])
-        for u in range(units):
+        rate_bank = bank(RATE_BANK, [P, UNITS, P])
+        for u in range(UNITS):
             nc.tensor.transpose(rate_bank[:, u, :], rate_rows[:, u * UNIT : (u + 1) * UNIT], ident[:])
-        rate = keep.tile([P, units, RUNS], F32, name="rate")
-        nc.vector.tensor_scalar(rate[:], rate_bank[:, :, 0:RUNS], -1.0 / LOSS, None, MULT)
-        loss_gain = keep.tile([P, PACK], F32, name="loss_gain")
-        nc.vector.tensor_scalar(loss_gain[:], gain[:], -LOSS, None, MULT)
-        w3_q = quantize(cast_weight(0, w3_raw, "w3", 28672), N, "w3", 1)
+        rate = keep.tile([P, UNITS, RUNS], F32, name="rate")
+        nc.scalar.activation(rate[:], rate_bank[:, :, 0:RUNS], COPY, scale=-1.0 / LOSS)
+        gains = []
+        for place in (GAIN_AT, HELD_AT):
+            factor = placed([P, PACK], F32, "gain_at_%d" % place, place)
+            nc.scalar.activation(factor[:], gain[:], COPY, scale=-LOSS)
+            gains.append(factor)
+        w3_q = quantize_on_vector(w3_raw, "w3", W3_AT)
 
-        def front(u):
-            lcols = slice(u * UNIT // 16, (u + 1) * UNIT // 16)
-            g = shared.tile([P, 2, PACK, UNIT], F32, name="g%d" % u, offset=(8192, 8192, 16384, 17408)[u], align_bytes=64)
-            contacts = bank(0, [P, PACK, P])
-            for t in range(PACK):
-                nc.scalar.activation(g[:, 0, t, :], logits[t][:].indirect(e1_l[:, lcols]), SIGMOID)
-                nc.scalar.activation(g[:, 1, t, :], logits[t][:].indirect(e2_l[:, lcols]), SIGMOID)
-                turned_sum(contacts[:, t, :], g[:, 0, t, :], g[:, 1, t, :])
+        def turned_terms(u):
+            shares = placed([P, 2, PACK, UNIT], F32, "shares%d" % u, SHARES_AT[u])
             if u > 0:
-                susceptible(u)
+                y_logits(u)
+            if u > 1:
                 for t in range(PACK):
                     turn_logits(u, t)
-            y = shared.tile([P, PACK, P], F32, name="y%d" % u, offset=(0, 19456, 20480, 21504)[u], align_bytes=64)
+            contacts = bank(CONTACTS_BANK, [P, PACK, P])
+            for t in range(PACK):
+                for k, list_tile in enumerate((e1_l, e2_l)):
+                    nc.scalar.activation(shares[:, k, t, :], logits[t][:].indirect(entries(list_tile, u * UNIT, UNIT)), SIGMOID)
+                turn(contacts[:, t, :], shares[:, 0, t, :], True, False)
+                turn(contacts[:, t, :], shares[:, 1, t, :], False, True)
+            y = placed([P, PACK, P], F32, "y%d" % u, Y_AT[u])
             nc.scalar.activation(y[:].rearrange("p t m -> p (t m)"), y_banks[u][:], SIGMOID)
-            c = ring.tile([P, PACK, P], F32, name="c", bufs=1)
+            c = placed([P, PACK, P], F32, "c%d" % u, C_AT[u])
             nc.scalar.activation(c[:], c_banks[u][:], SIGMOID)
-            cases = ring.tile([P, PACK, P], F32, name="cases")
+            cases = placed([P, PACK, P], F32, "cases%d" % u, CASES_AT[u])
             for r in range(RUNS):
-                run = slice(16 * r, 16 * r + 16)
+                run = slice(GROUP * r, GROUP * (r + 1))
                 nc.vector.scalar_tensor_tensor(cases[:, :, run], contacts[:, :, run], rate[:, u, r : r + 1], y[:, :, run], MULT, MULT)
             return c, cases
 
-        def back(u, c, cases):
-            total = bank(1, [P, PACK, UNIT])
-            terms = (c, cases) if u != 1 else (cases, c)
+        def quantized_z(u, c, cases):
+            total = bank(TOTAL_BANK if u < LAST else RATE_BANK, [P, PACK, UNIT])
+            terms = (c, cases) if u in (0, LAST) else (cases, c)
             for k, term in enumerate(terms):
                 for t in range(PACK):
-                    nc.tensor.matmul(
-                        total[:, t, :], term[:, t, :], ident[:], start=(k, t) == (0, 0), stop=(k, t) == (1, PACK - 1), is_transpose=True
-                    )
-            z = keep.tile([P, UNIT * PACK], BF16, name="z%d" % u, align_bytes=64)
-            if u == 3:
-                scaled = keep.tile([P, PACK, UNIT], BF16, name="scaled%d" % u)
-                for t in range(PACK):
-                    nc.scalar.activation(scaled[:, t, :], total[:, t, :], COPY, scale=loss_gain[:, t : t + 1])
-                nc.scalar.copy(out=z[:].rearrange("p (b i t) -> p b t i", i=4, t=PACK), in_=scaled[:].rearrange("p t (b i) -> p b t i", i=4))
-            else:
-                nc.vector.tensor_tensor(
-                    z[:].rearrange("p (j t) -> p j t", t=PACK),
-                    total[:].rearrange("p t j -> p j t"),
-                    loss_gain[:].unsqueeze(1).to_broadcast([P, UNIT, PACK]),
-                    MULT,
-                )
+                    turn(total[:, t, :], term[:, t, :], (k, t) == (0, 0), (k, t) == (1, PACK - 1))
+            z = placed([P, UNIT * PACK], BF16, "z%d" % u, Z_AT[u])
+            nc.vector.tensor_tensor(
+                z[:].rearrange("p (j t) -> p j t", t=PACK),
+                total[:].rearrange("p t j -> p j t"),
+                gains[u // LAST][:].unsqueeze(1).to_broadcast([P, UNIT, PACK]),
+                MULT,
+            )
             return quantize(z, UNIT, "z%d" % u, 1)
 
-        def scatter(t, h, j0, n):
-            nc.vector.tensor_copy(pages[t][:].indirect(slot_l[:, j0 // 16 : (j0 + n) // 16]), h)
+        def results(u, first, count, number):
+            acc = bank(number, [P, count, UNIT])
+            for k in range(count):
+                product(acc[:, k, :], w3_q, quarter(first + k), z_q[u], slice(0, UNIT))
+            return acc
 
-        def write(u, z_q, groups, number, spare=None):
-            tiles = [t for group in groups for t in group]
-            acc = bank(number, [P, len(tiles), UNIT])
-            for k, t in enumerate(tiles):
-                product(acc[:, k, :], w3_q, slice(t * P, (t + 1) * P), z_q, slice(0, UNIT))
-            for group in groups:
-                k0 = tiles.index(group[0])
-                if spare is not None and group == (PACK - 1,):
-                    nc.scalar.copy(out=spare, in_=acc[:, k0, :])
-                    continue
-                h = keep.tile([P, len(group), UNIT], F32, name="h%d_%d" % (u, group[0]))
-                nc.scalar.copy(out=h[:], in_=acc[:, k0 : k0 + len(group), :])
-                for k, t in enumerate(group):
-                    scatter(t, h[:, k, :], u * UNIT, UNIT)
+        def scatter(t, values, j0, n):
+            nc.vector.tensor_copy(pages[t][:].indirect(entries(slot_l, j0, n)), values)
+
+        def write(u, first, part, h):
+            nc.scalar.copy(out=h[:], in_=part)
+            for k in range(h.shape[1]):
+                scatter(first + k, h[:, k, :], u * UNIT, UNIT)
+
+        def write_fresh(u, first, part):
+            write(u, first, part, keep.tile([P, part.shape[1], UNIT], F32, name="h%d_%d" % (u, first)))
 
         z_q = {}
-        last = units - 1
         both = keep.tile([P, 2 * UNIT], F32, name="both")
-        ahead = front(0)
-        for u in range(units):
-            z_q[u] = back(u, *ahead)
+        terms = turned_terms(0)
+        for u in range(LAST):
+            z_q[u] = quantized_z(u, *terms)
             if u == 0:
-                x_idx.append(pick(offs_l, S // 2, S // 2, "x_idx1", (0, 1024)))
-            if u < last:
-                ahead = front(u + 1)
-            if 0 < u < last:
-                write(u - 1, z_q[u - 1], ((3,),), 1)
-            if u < last - 1:
-                write(u, z_q[u], ((0,), (1, 2)), 3)
-            if u == last - 1:
-                write(u, z_q[u], ((0,), (1,)), 3)
-        write(last - 1, z_q[last - 1], ((2,), (3,)), 1, both[:, :UNIT])
-        write(last, z_q[last], ((0,), (1, 2), (3,)), 3, both[:, UNIT:])
-        scatter(PACK - 1, both[:], (last - 1) * UNIT, 2 * UNIT)
+                x_idx.append(pick(offs_l, S // 2, S // 2, "x_idx1", IDX_LATE_WORDS, IDX_LATE_BYTES))
+            terms = turned_terms(u + 1)
+            if u > 0:
+                write_fresh(u - 1, 3, results(u - 1, 3, 1, TOTAL_BANK)[:])
+            write_fresh(u, 0, results(u, 0, 1, FIRST_BANK)[:])
+            if u < LAST - 1:
+                write_fresh(u, 1, results(u, 1, 2, MIDDLE_BANK)[:])
+
+        rest = results(LAST - 1, 1, 3, MIDDLE_BANK)
+        nc.scalar.copy(out=both[:, :UNIT], in_=rest[:, 2, :])
+        z_q[LAST] = quantized_z(LAST, *terms)
+        write(LAST - 1, 1, rest[:, 0:2, :], placed([P, 2, UNIT], F32, "held", HELD_AT))
+        final = results(LAST, 0, PACK, TOTAL_BANK)
+        write_fresh(LAST, 0, final[:, 0:1, :])
+        write_fresh(LAST, 1, final[:, 1:3, :])
+        nc.scalar.copy(out=both[:, UNIT:], in_=final[:, 3, :])
+        scatter(PACK - 1, both[:], (LAST - 1) * UNIT, 2 * UNIT)
         for t in range(PACK):
             nc.sync.dma_start(out.rearrange("(p t) u -> p t u", t=PACK)[:, t, :], pages[t][:])

from contextlib import ExitStack

import concourse.mybir as mybir
from concourse.masks import make_identity

K, T, S, N, H, U = 512, 2048, 512, 512, 512, 1024
RUNS = 8
FLOPS = 2 * K * H * S * 2 + 2 * H * N * S
BYTES = K * T + K * T // 32 + 4 * (2 * K * H + H * N) + 4 * RUNS * S + 4 * H + 2 * 4 * N * U + 5 * 2 * 128 * S // 16

F32 = mybir.dt.float32
BF16 = mybir.dt.bfloat16
I32 = mybir.dt.int32
U32 = mybir.dt.uint32
U16 = mybir.dt.uint16
U8 = mybir.dt.uint8
FP8X4 = mybir.dt.float8_e4m3fn_x4
MULT = mybir.AluOpType.mult
COPY = mybir.ActivationFunctionType.Copy
SIGMOID = mybir.ActivationFunctionType.Sigmoid

P = 128
PACK = 4
UNIT = 128
UNITS = S // UNIT
LAST = UNITS - 1
GROUP = 16
LOSS = 0.75
W2_SCALAR_SHARE = 44

KB = 1024
Y_FIRST = 0
IDX_LATE_WORDS, IDX_LATE_BYTES = Y_FIRST, Y_FIRST + KB
TWO_WORDS, TWO_BYTES, IDX_EARLY_BYTES = 4 * KB, 6 * KB, 7 * KB + 512
C_FIRST = 8 * KB
SHARES_AT = (9 * KB, 10 * KB, 16 * KB, 17 * KB)
Y_AT = (Y_FIRST, 19 * KB, 20 * KB, 21 * KB)
W2_AT, W1_AT = 24 * KB, 28 * KB
IDX_EARLY_WORDS, W3_AT, CASES_FIRST = W2_AT, W1_AT, W1_AT
GAIN_AT = 36 * KB
HELD_AT = GAIN_AT + KB
Z_AT = tuple(42 * KB + 4 * KB * u for u in range(UNITS))
C_AT = (C_FIRST, Z_AT[0] + KB // 2 - 2 * KB, Z_AT[1] + KB // 2 - 2 * KB, SHARES_AT[LAST])
CASES_AT = (CASES_FIRST, Z_AT[0] + KB // 2, Z_AT[1] + KB // 2, Z_AT[2] + KB // 2)

CONTACTS_BANK = 0
TOTAL_BANK = 1
FIRST_BANK = 2
MIDDLE_BANK = 3
RATE_BANK = 4
Y_BANK = 5
TURNED_BANK = 6
TURNED_FIRST_BANK = 7


def tile_picked_sirstep_none_p_kernel(tc, x_words, x_scales, w1, w2, beta, gn, w3, mem, offs, two, e1, e2, slot, out):
    nc = tc.nc
    with ExitStack() as ctx:
        keep = ctx.enter_context(tc.tile_pool(name="keep", bufs=1))
        shared = ctx.enter_context(tc.tile_pool(name="shared", bufs=1))
        psum = ctx.enter_context(tc.psum_pool(name="psum", bufs=1))

        def bank(number, shape):
            return psum.tile(shape, F32, name="bank%d" % number)

        def placed(shape, dtype, name, place):
            return shared.tile(shape, dtype, name=name, offset=place, align_bytes=64)

        def entries(list_tile, j0, n):
            return list_tile[:, j0 // GROUP : (j0 + n) // GROUP]

        def load_list(dram, name):
            tile = keep.tile([P, S // GROUP], U16, name=name)
            nc.sync.dma_start(tile[:], dram)
            return tile

        def load_weight(dram, name):
            raw = keep.tile([P, PACK, dram.shape[1]], F32, name=name + "_raw")
            nc.sync.dma_start(raw[:], dram.rearrange("(p j) c -> p j c", j=PACK))
            return raw

        def cast_views(raw, name, place):
            grouped = placed([P, PACK * H], BF16, name + "_bf16", place)
            dealt = grouped[:].rearrange("p (t m j) -> p m t j", t=PACK, j=PACK)
            return grouped, dealt, raw[:].rearrange("p j (m t) -> p m t j", t=PACK)

        def quantize(grouped, width, name, pieces):
            codes = keep.tile([P, width], U32, name=name + "_codes", align_bytes=64)
            scales = keep.tile([P, width], U8, name=name + "_scales", align_bytes=64)
            piece = width // pieces
            for c0 in range(0, width, piece):
                nc.vector.quantize_mx(
                    out=codes[:, c0 : c0 + piece].bitcast(FP8X4),
                    scales=scales[:, c0 : c0 + piece],
                    in_=grouped[:, PACK * c0 : PACK * (c0 + piece)],
                )
            return codes, scales

        def quantize_on_vector(raw, name, place):
            grouped, dealt, source = cast_views(raw, name, place)
            nc.vector.tensor_copy(out=dealt, in_=source)
            return quantize(grouped, H, name, 1)

        def product(acc, still, still_cols, moving, moving_cols):
            nc.tensor.matmul_mx(
                out=acc,
                lhsT=still[0][:, still_cols].bitcast(FP8X4),
                lhsT_scale=still[1][:, still_cols],
                rhs=moving[0][:, moving_cols].bitcast(FP8X4),
                rhs_scale=moving[1][:, moving_cols],
                start=True,
                stop=True,
            )

        def turn(acc, block, start, stop):
            nc.tensor.matmul(acc, block, ident[:], start=start, stop=stop, is_transpose=True)

        def quarter(t):
            return slice(t * P, (t + 1) * P)

        x_table = keep.tile([P, T], U32, name="x_table")
        x_bytes = keep.tile([P, T], U8, name="x_bytes")
        nc.vector.memset(x_bytes[:].bitcast(I32), 0)
        warm = keep.tile([P, 2], F32, name="warm")
        nc.vector.memset(warm[:, 0:1], 0.0)
        rate_rows = keep.tile([P, S], F32, name="rate_rows")
        nc.gpsimd.memset(rate_rows[:], 0.0)
        ident = keep.tile([P, P], F32, name="ident")
        make_identity(nc, ident[:])

        x_rows = keep.tile([P, T], U8, name="x_rows")
        for q in range(4):
            nc.sync.dma_start(x_rows[32 * q : 32 * q + 4, :].bitcast(I32), x_scales[0, 4 * q : 4 * q + 4, :].bitcast(I32))
        two_l = load_list(two, "two_l")
        nc.sync.dma_start(x_table[:].bitcast(I32), x_words[0].rearrange("p n t -> p (n t)").bitcast(I32))
        offs_l = load_list(offs, "offs_l")
        for q in range(4):
            nc.vector.tensor_copy(x_bytes[32 * q : 32 * q + 4, :].bitcast(I32), x_rows[32 * q : 32 * q + 4, :].bitcast(I32))
        nc.scalar.activation(warm[:, 1:2], warm[:, 0:1], SIGMOID)
        w2_raw = load_weight(w2, "w2")
        gain = keep.tile([P, PACK], F32, name="gain")
        nc.sync.dma_start(gain[:], gn.rearrange("(p t) o -> p (t o)", t=PACK))
        nc.sync.dma_start(rate_rows[0:RUNS, :], beta.rearrange("(r x) s -> r x s", r=RUNS)[:, 0, :])
        w1_raw = load_weight(w1, "w1")
        e1_l = load_list(e1, "e1_l")
        e2_l = load_list(e2, "e2_l")
        w3_raw = load_weight(w3, "w3")
        slot_l = load_list(slot, "slot_l")
        pages = []
        for t in range(PACK):
            page = keep.tile([P, U], F32, name="page%d" % t)
            nc.sync.dma_start(page[:], mem.rearrange("(p t) u -> p t u", t=PACK)[:, t, :])
            pages.append(page)

        def pick(list_tile, j0, n, name, words_at, bytes_at):
            words = placed([P, n], U32, name + "_words", words_at)
            scale_bytes = placed([P, n], U8, name + "_bytes", bytes_at)
            nc.vector.tensor_copy(scale_bytes[:], x_bytes[:].indirect(entries(list_tile, j0, n)))
            nc.vector.tensor_copy(words[:], x_table[:].indirect(entries(list_tile, j0, n)))
            return words, scale_bytes

        x_two = pick(two_l, 0, S, "x_two", TWO_WORDS, TWO_BYTES)
        grouped, dealt, source = cast_views(w2_raw, "w2", W2_AT)
        nc.scalar.copy(out=dealt[:, :W2_SCALAR_SHARE], in_=source[:, :W2_SCALAR_SHARE])
        nc.vector.tensor_copy(out=dealt[:, W2_SCALAR_SHARE:], in_=source[:, W2_SCALAR_SHARE:])
        w2_q = quantize(grouped, H, "w2", 2)

        x_idx = [pick(offs_l, 0, S // 2, "x_idx0", IDX_EARLY_WORDS, IDX_EARLY_BYTES)]
        w1_q = quantize_on_vector(w1_raw, "w1", W1_AT)

        y_banks = {}
        c_banks = {}
        logits = []

        def y_logits(u):
            y_banks[u] = bank(Y_BANK if u < 2 else FIRST_BANK, [P, H])
            product(y_banks[u][:], x_idx[u // 2], slice(u % 2 * UNIT, (u % 2 + 1) * UNIT), w1_q, slice(0, H))

        def turn_logits(u, t):
            if t == 0:
                c_banks[u] = bank(TURNED_BANK if u > 0 else TURNED_FIRST_BANK, [P, PACK, P])
            nc.tensor.transpose(c_banks[u][:, t, :], logits[t][:, u * UNIT : (u + 1) * UNIT], ident[:])

        y_logits(0)
        for t in range(PACK):
            acc = bank(t, [P, S])
            product(acc[:], w2_q, quarter(t), x_two, slice(0, S))
            logit = keep.tile([P, S], F32, name="logit%d" % t)
            (nc.scalar.copy if t < 2 else nc.vector.tensor_copy)(out=logit[:], in_=acc[:])
            logits.append(logit)
            turn_logits(0, t)
            turn_logits(1, t)

        rate_bank = bank(RATE_BANK, [P, UNITS, P])
        for u in range(UNITS):
            nc.tensor.transpose(rate_bank[:, u, :], rate_rows[:, u * UNIT : (u + 1) * UNIT], ident[:])
        rate = keep.tile([P, UNITS, RUNS], F32, name="rate")
        nc.scalar.activation(rate[:], rate_bank[:, :, 0:RUNS], COPY, scale=-1.0 / LOSS)
        gains = []
        for place in (GAIN_AT, HELD_AT):
            factor = placed([P, PACK], F32, "gain_at_%d" % place, place)
            nc.scalar.activation(factor[:], gain[:], COPY, scale=-LOSS)
            gains.append(factor)
        w3_q = quantize_on_vector(w3_raw, "w3", W3_AT)

        def turned_terms(u):
            shares = placed([P, 2, PACK, UNIT], F32, "shares%d" % u, SHARES_AT[u])
            if u > 0:
                y_logits(u)
            if u > 1:
                for t in range(PACK):
                    turn_logits(u, t)
            contacts = bank(CONTACTS_BANK, [P, PACK, P])
            for t in range(PACK):
                for k, list_tile in enumerate((e1_l, e2_l)):
                    nc.scalar.activation(shares[:, k, t, :], logits[t][:].indirect(entries(list_tile, u * UNIT, UNIT)), SIGMOID)
                turn(contacts[:, t, :], shares[:, 0, t, :], True, False)
                turn(contacts[:, t, :], shares[:, 1, t, :], False, True)
            y = placed([P, PACK, P], F32, "y%d" % u, Y_AT[u])
            nc.scalar.activation(y[:].rearrange("p t m -> p (t m)"), y_banks[u][:], SIGMOID)
            c = placed([P, PACK, P], F32, "c%d" % u, C_AT[u])
            nc.scalar.activation(c[:], c_banks[u][:], SIGMOID)
            cases = placed([P, PACK, P], F32, "cases%d" % u, CASES_AT[u])
            for r in range(RUNS):
                run = slice(GROUP * r, GROUP * (r + 1))
                nc.vector.scalar_tensor_tensor(cases[:, :, run], contacts[:, :, run], rate[:, u, r : r + 1], y[:, :, run], MULT, MULT)
            return c, cases

        def quantized_z(u, c, cases):
            total = bank(TOTAL_BANK if u < LAST else RATE_BANK, [P, PACK, UNIT])
            terms = (c, cases) if u in (0, LAST) else (cases, c)
            for k, term in enumerate(terms):
                for t in range(PACK):
                    turn(total[:, t, :], term[:, t, :], (k, t) == (0, 0), (k, t) == (1, PACK - 1))
            z = placed([P, UNIT * PACK], BF16, "z%d" % u, Z_AT[u])
            nc.vector.tensor_tensor(
                z[:].rearrange("p (j t) -> p j t", t=PACK),
                total[:].rearrange("p t j -> p j t"),
                gains[u // LAST][:].unsqueeze(1).to_broadcast([P, UNIT, PACK]),
                MULT,
            )
            return quantize(z, UNIT, "z%d" % u, 1)

        def results(u, first, count, number):
            acc = bank(number, [P, count, UNIT])
            for k in range(count):
                product(acc[:, k, :], w3_q, quarter(first + k), z_q[u], slice(0, UNIT))
            return acc

        def scatter(t, values, j0, n):
            nc.vector.tensor_copy(pages[t][:].indirect(entries(slot_l, j0, n)), values)

        def write(u, first, part, h):
            nc.scalar.copy(out=h[:], in_=part)
            for k in range(h.shape[1]):
                scatter(first + k, h[:, k, :], u * UNIT, UNIT)

        def write_fresh(u, first, part):
            write(u, first, part, keep.tile([P, part.shape[1], UNIT], F32, name="h%d_%d" % (u, first)))

        z_q = {}
        both = keep.tile([P, 2 * UNIT], F32, name="both")
        terms = turned_terms(0)
        for u in range(LAST):
            z_q[u] = quantized_z(u, *terms)
            if u == 0:
                x_idx.append(pick(offs_l, S // 2, S // 2, "x_idx1", IDX_LATE_WORDS, IDX_LATE_BYTES))
            terms = turned_terms(u + 1)
            if u > 0:
                write_fresh(u - 1, 3, results(u - 1, 3, 1, TOTAL_BANK)[:])
            write_fresh(u, 0, results(u, 0, 1, FIRST_BANK)[:])
            if u < LAST - 1:
                write_fresh(u, 1, results(u, 1, 2, MIDDLE_BANK)[:])

        rest = results(LAST - 1, 1, 3, MIDDLE_BANK)
        nc.scalar.copy(out=both[:, :UNIT], in_=rest[:, 2, :])
        z_q[LAST] = quantized_z(LAST, *terms)
        write(LAST - 1, 1, rest[:, 0:2, :], placed([P, 2, UNIT], F32, "held", HELD_AT))
        final = results(LAST, 0, PACK, TOTAL_BANK)
        write_fresh(LAST, 0, final[:, 0:1, :])
        write_fresh(LAST, 1, final[:, 1:3, :])
        nc.scalar.copy(out=both[:, UNIT:], in_=final[:, 3, :])
        scatter(PACK - 1, both[:], (LAST - 1) * UNIT, 2 * UNIT)
        for t in range(PACK):
            nc.sync.dma_start(out.rearrange("(p t) u -> p t u", t=PACK)[:, t, :], pages[t][:])
